import numpy as np
import ml_dtypes


def mxq(x, axis, fmt="e4m3"):
    dtype, down = {"e4m3": (ml_dtypes.float8_e4m3fn, 7), "e5m2": (ml_dtypes.float8_e5m2, 14)}[fmt]
    v = np.moveaxis(np.asarray(x, np.float32).astype(ml_dtypes.bfloat16).astype(np.float64), axis, -1)
    blocks = v.reshape(v.shape[:-1] + (-1, 32))
    amax = np.abs(blocks).max(-1, keepdims=True)
    byte = np.maximum(np.where(amax > 0, np.frexp(amax)[1] - 1 + 127, 0) - down, 1)
    scale = np.exp2(byte - 127.0)
    codes = (blocks / scale).astype(np.float32).astype(dtype).astype(np.float64)
    return np.moveaxis((codes * scale).reshape(v.shape), -1, axis)


WIDE = False


def mx_kscale(k):
    if not WIDE:
        return np.ones(k)
    levels = np.array([10, -10, 5, -5, 0])
    if k % 512:
        return np.exp2(np.random.permutation(np.resize(levels, k // 32))).repeat(32)
    a = np.empty((k // 512, 16))
    for p in range(k // 512):
        a[p, :8] = np.random.permutation(np.resize(levels, 8))
        for g in range(8):
            far = levels[np.abs(levels - a[p, g]) >= 10]
            a[p, g + 8] = far[np.random.randint(len(far))]
    return np.exp2(a.ravel()).repeat(32)


def f64(x):
    return np.asarray(x).astype(np.float64)


E2M1 = np.array([0.0, 0.5, 1.0, 1.5, 2.0, 3.0, 4.0, 6.0, -0.0, -0.5, -1.0, -1.5, -2.0, -3.0, -4.0, -6.0])


def pack_weight(w, fmt):
    k, n = w.shape
    w = f64(np.asarray(w, np.float32).astype(ml_dtypes.bfloat16)).reshape(k // 32, 32, n)
    amax = np.abs(w).max(1)
    if fmt == "e4m3":
        byte = np.frexp(amax)[1] - 1 + 127 - 7
    else:
        mant, ex = np.frexp(amax / 6.0)
        byte = np.where(mant > 0.5, ex, ex - 1) + 127
    byte = np.clip(np.where(amax > 0, byte, 1), 1, 254)
    scaled = (w * np.exp2(127.0 - byte)[:, None, :]).reshape(k, n).astype(np.float32)
    by_word = np.ascontiguousarray(scaled.reshape(k // 512, 128, 4, n).transpose(0, 1, 3, 2))
    if fmt == "e4m3":
        words = by_word.astype(ml_dtypes.float8_e4m3fn).view(np.uint8)
    else:
        c = by_word.astype(ml_dtypes.float4_e2m1fn).view(np.uint8) & 0xF
        words = (c[..., 0::2] | (c[..., 1::2] << 4)).reshape(k // 512, 128, 2 * n)
    return np.ascontiguousarray(words), np.ascontiguousarray(byte.astype(np.uint8).reshape(k // 512, 16, n))


def unpack_weight(words, scales, fmt):
    g, _, n = scales.shape
    words = np.ascontiguousarray(words).reshape(g, 128, n, -1)
    if fmt == "e4m3":
        vals = words.view(ml_dtypes.float8_e4m3fn).astype(np.float64)
    else:
        nib = np.empty((g, 128, n, 4), np.uint8)
        nib[..., 0::2] = words & 0xF
        nib[..., 1::2] = words >> 4
        vals = E2M1[nib]
    vals = vals * np.repeat(np.exp2(scales.astype(np.float64) - 127.0), 8, axis=1)[..., None]
    return vals.transpose(0, 1, 3, 2).reshape(g * 512, n)


def planes(y):
    n, m = y.shape
    v = y.astype(np.float32).astype(ml_dtypes.bfloat16).astype(np.float64).reshape(n // 32, 32, m)
    top = np.abs(v).max(1)
    byte = np.clip(np.where(top > 0, np.frexp(top)[1] - 1 + 127 - 7, 1), 1, 254)
    codes = (v * np.exp2(127.0 - byte)[:, None, :]).reshape(n, m).astype(np.float32).astype(ml_dtypes.float8_e4m3fn).view(np.uint8)
    words = codes.reshape(n // 512, 128, 4, m).transpose(0, 1, 3, 2)
    return np.ascontiguousarray(words), np.ascontiguousarray(byte.astype(np.uint8).reshape(n // 512, 16, m))


O, K, R, M, T = 512, 1536, 512, 1536, 512


def setup_inputs():
    n = np.random.standard_normal
    s = mx_kscale(K)[:, None]
    u = mx_kscale(R)[:, None]
    x = n((K, T)); x[:O] *= 6.0
    w = n((K, M)) / np.sqrt(K) / s; w[:O] /= 2.0
    p_w8 = pack_weight(w[:O], "e4m3")
    p_w4 = pack_weight(w[O:], "e2m1")
    p_up = pack_weight(n((R, M)) / np.sqrt(R) / u, "e2m1")
    return {
        "x": (x * s).astype(np.float32),
        "w8_words": p_w8[0],
        "w8_scales": p_w8[1],
        "w4_words": p_w4[0],
        "w4_scales": p_w4[1],
        "down": (0.3 * n((K, R)) / np.sqrt(K) / s * u.T).astype(np.float32),
        "up_words": p_up[0],
        "up_scales": p_up[1],
    }


def reference(x, w8_words, w8_scales, w4_words, w4_scales, down, up_words, up_scales):
    x_ = mxq(f64(x), 0, "e4m3")
    w8_ = unpack_weight(w8_words, w8_scales, "e4m3")
    w4_ = unpack_weight(w4_words, w4_scales, "e2m1")
    down_ = mxq(f64(down), 0, "e4m3")
    up_ = unpack_weight(up_words, up_scales, "e2m1")
    h_ = mxq(down_.T @ x_, 0, "e4m3")
    y = w8_.T @ x_[:O] + w4_.T @ x_[O:] + up_.T @ h_
    out_0 = np.maximum(y, 0.0) ** 2
    return (out_0,) + planes(out_0)

@@ -1,0 +1,348 @@
+from contextlib import ExitStack
+
+import concourse.mybir as mybir
+
+O, K, R, M, T = 512, 1536, 512, 1536, 512
+FLOPS = 2 * T * (K * R + K * M + R * M)
+
+F32 = mybir.dt.float32
+BF16 = mybir.dt.bfloat16
+I32 = mybir.dt.int32
+U8 = mybir.dt.uint8
+FP8X4 = mybir.dt.float8_e4m3fn_x4
+FP4X4 = mybir.dt.float4_e2m1fn_x4
+ACT = mybir.ActivationFunctionType
+ALU = mybir.AluOpType
+
+P = 128
+PACK = 4
+KP = P * PACK
+GROUPS = M // KP
+QUADS = 4
+HALF = T // 2
+TQ = T // 4
+W8_ROW = 4
+
+
+def tile_mix_three_fm_pl_relu2_kernel(
+    tc, x, w8_words, w8_scales, w4_words, w4_scales, down, up_words, up_scales, out_0, out_1, out_2
+):
+    nc = tc.nc
+    with ExitStack() as ctx:
+        sb = ctx.enter_context(tc.tile_pool(name="sb", bufs=1))
+        ps = ctx.enter_context(tc.psum_pool(name="ps", bufs=1))
+        ctx.enter_context(tc.manual_schedule())
+
+        def tiles(name, count, shape, dtype):
+            return [sb.tile(shape, dtype, name="%s%d" % (name, n), align_bytes=64) for n in range(count)]
+
+        banks = [ps.tile([P, T], F32, name="bank%d" % n) for n in range(8)]
+
+        x_raw = tiles("x_raw", 2, [P, PACK, T], F32)
+        x_last_raw = tiles("x_last_raw", 2, [P, PACK, HALF], F32)
+        d_raw = tiles("d_raw", 3, [P, PACK, R], F32)
+        x_bf = tiles("x_bf", 2, [P, T * PACK], BF16)
+        x_last_bf = tiles("x_last_bf", 2, [P, HALF * PACK], BF16)
+        d_bf = tiles("d_bf", 3, [P, R * PACK], BF16)
+        x_codes = tiles("x_codes", 3, [P, T], I32)
+        x_scale = tiles("x_scale", 3, [P, T], U8)
+        d_codes = tiles("d_codes", 3, [P, R], I32)
+        d_scale = tiles("d_scale", 3, [P, R], U8)
+        h_bf = tiles("h_bf", 2, [P, HALF * PACK], BF16)
+        h_codes = sb.tile([P, T], I32, align_bytes=64)
+        h_scale = sb.tile([P, T], U8, align_bytes=64)
+
+        w8_raw = tiles("w8_raw", GROUPS, [P, KP], I32)
+        w4_raw = tiles("w4_raw", GROUPS, [P, 2, 2 * KP], U8)
+        up_raw = tiles("up_raw", GROUPS, [P, 2 * KP], U8)
+        w8_dealt = tiles("w8_dealt", GROUPS, [P, KP], I32)
+        w4_dealt = tiles("w4_dealt", GROUPS, [P, 2, 2 * KP], U8)
+        up_dealt = tiles("up_dealt", GROUPS, [P, 2 * KP], U8)
+        w4_s_raw = sb.tile([P, 2, M], U8, align_bytes=64)
+        up8_s_raw = sb.tile([P, M], U8, align_bytes=64)
+        w4_s = tiles("w4_s", 2, [P, M], U8)
+        up8_s = sb.tile([P, M], U8, align_bytes=64)
+
+        o_f32 = tiles("o_f32", GROUPS, [P, PACK, T], F32)
+        o_bf = tiles("o_bf", 2 * GROUPS, [P, HALF * PACK], BF16)
+        o_codes = tiles("o_codes", GROUPS, [P, T], I32)
+        o_scale = sb.tile([P, GROUPS * T], U8, align_bytes=64)
+
+        def rows(src, c):
+            return src[c * KP : (c + 1) * KP, :].rearrange("(p j) w -> p j w", j=PACK)
+
+        w8_src = w8_words[0].rearrange("p n i -> p (n i)")
+        w4_src = w4_words.rearrange("g p b -> p g b")
+
+        def load_w8(a):
+            nc.sync.dma_start(out=w8_raw[a][:], in_=w8_src[:, a * 4 * KP : (a + 1) * 4 * KP].bitcast(I32))
+
+        def load_w4(a):
+            nc.sync.dma_start(out=w4_raw[a][:].bitcast(I32), in_=w4_src[:, :, a * 2 * KP : (a + 1) * 2 * KP].bitcast(I32))
+
+        def load_up(a):
+            nc.sync.dma_start(out=up_raw[a][:].bitcast(I32), in_=up_words[0][:, a * 2 * KP : (a + 1) * 2 * KP].bitcast(I32))
+
+        def x_views(raw, bf, lo, hi):
+            dst = bf[:, lo * PACK : hi * PACK].rearrange("p (c i j) -> p c j i", i=4, j=PACK)
+            src = raw[:, :, lo:hi].rearrange("p j (c i) -> p c j i", i=4)
+            return dst, src
+
+        def d_views(raw, bf, lo, hi):
+            dst = bf[:].rearrange("p (s m j) -> p m j s", s=PACK, j=PACK)[:, lo // PACK : hi // PACK]
+            src = raw[:, :, lo:hi].rearrange("p j (m s) -> p m j s", s=PACK)
+            return dst, src
+
+        def cast_scalar(views, raw, bf, lo, hi):
+            dst, src = views(raw, bf, lo, hi)
+            nc.scalar.copy(out=dst, in_=src)
+
+        def cast_vector(views, raw, bf, lo, hi):
+            dst, src = views(raw, bf, lo, hi)
+            nc.vector.tensor_copy(out=dst, in_=src)
+
+        def cast_shared(views, raw, bf):
+            width = raw.shape[2]
+            cut = 3 * width // 8
+            cast_scalar(views, raw, bf, 0, cut)
+            cast_vector(views, raw, bf, cut, width)
+
+        def quantize(bf, codes, scale):
+            nc.vector.quantize_mx(out=codes.bitcast(FP8X4), scales=scale, in_=bf[:])
+
+        def deal_scale(dst, src):
+            nc.vector.tensor_copy(
+                out=dst.rearrange("p (a s m) -> p s a m", a=GROUPS, s=PACK),
+                in_=src.rearrange("p (a m s) -> p s a m", a=GROUPS, s=PACK),
+            )
+
+        def deal_w8(a):
+            nc.vector.tensor_copy(
+                out=w8_dealt[a][:].rearrange("p (s m) -> p m s", s=PACK),
+                in_=w8_raw[a][:].rearrange("p (m s) -> p m s", s=PACK),
+            )
+
+        def deal_w4(a):
+            nc.vector.tensor_copy(
+                out=w4_dealt[a][:].rearrange("p g (s m b) -> p g s m b", s=PACK, b=2),
+                in_=w4_raw[a][:].rearrange("p g (m s b) -> p g s m b", s=PACK, b=2),
+            )
+
+        def deal_up(a):
+            nc.vector.tensor_copy(
+                out=up_dealt[a][:].rearrange("p (s m b) -> p s m b", s=PACK, b=2),
+                in_=up_raw[a][:].rearrange("p (m s b) -> p s m b", s=PACK, b=2),
+            )
+
+        def h_pass(c, q):
+            for s in range(PACK):
+                nc.tensor.matmul_mx(
+                    out=banks[4 + q][:, s * P : (s + 1) * P],
+                    lhsT=d_codes[c][:, s * P : (s + 1) * P].bitcast(FP8X4),
+                    lhsT_scale=d_scale[c][:, s * P : (s + 1) * P],
+                    rhs=x_codes[c][:, q * TQ : (q + 1) * TQ].bitcast(FP8X4),
+                    rhs_scale=x_scale[c][:, q * TQ : (q + 1) * TQ],
+                    start=(c == 0 and s == 0),
+                    stop=(c == 2 and s == PACK - 1),
+                )
+
+        def h_views(q):
+            dst = h_bf[q // 2][:, (q % 2) * TQ * PACK : (q % 2 + 1) * TQ * PACK].rearrange("p (t s) -> p t s", s=PACK)
+            return dst, banks[4 + q][:].rearrange("p (s t) -> p t s", s=PACK)
+
+        def h_out_scalar(q):
+            dst, src = h_views(q)
+            nc.scalar.copy(out=dst, in_=src)
+
+        def h_out_vector(q):
+            dst, src = h_views(q)
+            nc.vector.tensor_copy(out=dst, in_=src)
+
+        def y_bank(a, s):
+            return banks[4 * (a % 2) + s]
+
+        def y_pass(a, s, n):
+            cols = slice(a * KP + s * P, a * KP + (s + 1) * P)
+            pair = slice(2 * s * P, 2 * (s + 1) * P)
+            if n == 0:
+                lhs, lhs_scale = w8_dealt[a][:, s * P : (s + 1) * P].bitcast(FP8X4), up8_s[W8_ROW:P, cols]
+            elif n < 3:
+                lhs, lhs_scale = w4_dealt[a][:, n - 1, pair].bitcast(FP4X4), w4_s[n - 1][:, cols]
+            else:
+                lhs, lhs_scale = up_dealt[a][:, pair].bitcast(FP4X4), up8_s[:, cols]
+            codes, scale = (x_codes[n], x_scale[n]) if n < 3 else (h_codes, h_scale)
+            nc.tensor.matmul_mx(
+                out=y_bank(a, s)[:],
+                lhsT=lhs,
+                lhsT_scale=lhs_scale,
+                rhs=codes[:].bitcast(FP8X4),
+                rhs_scale=scale[:],
+                start=(n == 0),
+                stop=(n == 3),
+            )
+
+        def relu_scalar(a, s):
+            nc.scalar.activation(out=o_f32[a][:, s, :], in_=y_bank(a, s)[:], func=ACT.Relu)
+
+        def relu_vector(a, s):
+            nc.vector.tensor_scalar(out=o_f32[a][:, s, :], in0=y_bank(a, s)[:], scalar1=0.0, scalar2=None, op0=ALU.max)
+
+        def square(a, s):
+            nc.scalar.activation(out=o_f32[a][:, s, :], in_=o_f32[a][:, s, :], func=ACT.Square)
+
+        def out_cast(a, u):
+            dst = o_bf[2 * a + u][:].rearrange("p (c i j) -> p c j i", i=4, j=PACK)
+            src = o_f32[a][:, :, u * HALF : (u + 1) * HALF].rearrange("p j (c i) -> p c j i", i=4)
+            nc.vector.tensor_copy(out=dst, in_=src)
+
+        def out_quantize(a, u):
+            quantize(
+                o_bf[2 * a + u],
+                o_codes[a][:, u * HALF : (u + 1) * HALF],
+                o_scale[:, a * T + u * HALF : a * T + (u + 1) * HALF],
+            )
+
+        def planes(a):
+            for u in range(2):
+                out_cast(a, u)
+            for u in range(2):
+                out_quantize(a, u)
+
+        def store_f32(a, lo, hi):
+            nc.sync.dma_start(out=rows(out_0, a)[:, lo:hi, :], in_=o_f32[a][:, lo:hi, :])
+
+        def store_codes(a, lo, hi):
+            dst = out_1[a].rearrange("p t i -> p (t i)")[:, lo * PACK : hi * PACK].bitcast(I32)
+            nc.sync.dma_start(out=dst, in_=o_codes[a][:, lo:hi])
+
+        def store_scale_rows(queue, q):
+            src = o_scale[32 * q : 32 * q + 4, :].bitcast(I32).rearrange("r (a w) -> r a w", a=GROUPS)
+            queue.dma_start(out=out_2[:, 4 * q : 4 * q + 4, :].rearrange("a r t -> r a t").bitcast(I32), in_=src)
+
+        def load_w4_scale(q):
+            nc.sync.dma_start(
+                out=w4_s_raw[32 * q : 32 * q + 4].bitcast(I32),
+                in_=w4_scales[:, 4 * q : 4 * q + 4, :].rearrange("g r n -> r g n").bitcast(I32),
+            )
+
+        def load_up8_scale(src, row, q):
+            nc.sync.dma_start(
+                out=up8_s_raw[32 * q + row : 32 * q + row + 4, :].bitcast(I32),
+                in_=src[0, 4 * q : 4 * q + 4, :].bitcast(I32),
+            )
+
+        nc.vector.memset(w4_s_raw[:].bitcast(I32), 0)
+        nc.vector.memset(up8_s_raw[:].bitcast(I32), 0)
+        nc.sync.dma_start(out=x_raw[0][:], in_=rows(x, 0))
+        for q in range(QUADS):
+            load_w4_scale(q)
+        for q in range(2):
+            load_up8_scale(w8_scales, W8_ROW, q)
+        nc.sync.dma_start(out=d_raw[0][:], in_=rows(down, 0))
+        nc.sync.dma_start(out=x_raw[1][:], in_=rows(x, 1))
+        for q in range(2, QUADS):
+            load_up8_scale(w8_scales, W8_ROW, q)
+        for q in range(QUADS):
+            load_up8_scale(up_scales, 0, q)
+        nc.sync.dma_start(out=d_raw[1][:], in_=rows(down, 1))
+        load_w8(0)
+        load_w4(0)
+        load_up(0)
+        nc.sync.dma_start(out=d_raw[2][:], in_=rows(down, 2))
+        for u in range(2):
+            nc.sync.dma_start(out=x_last_raw[u][:], in_=rows(x, 2)[:, :, u * HALF : (u + 1) * HALF])
+        for a in range(1, GROUPS):
+            load_w8(a)
+            load_w4(a)
+            load_up(a)
+
+        cast_scalar(x_views, x_raw[0], x_bf[0], 0, T)
+        for g in range(2):
+            deal_scale(w4_s[g][:], w4_s_raw[:, g, :])
+        quantize(x_bf[0], x_codes[0][:], x_scale[0][:])
+        cast_shared(d_views, d_raw[0], d_bf[0])
+        quantize(d_bf[0], d_codes[0][:], d_scale[0][:])
+        for q in range(QUADS):
+            h_pass(0, q)
+
+        cast_shared(x_views, x_raw[1], x_bf[1])
+        deal_scale(up8_s[:], up8_s_raw[:])
+        quantize(x_bf[1], x_codes[1][:], x_scale[1][:])
+        cast_scalar(d_views, d_raw[1], d_bf[1], 0, R)
+        deal_w8(0)
+        deal_w4(0)
+        quantize(d_bf[1], d_codes[1][:], d_scale[1][:])
+        for n in range(2):
+            for s in range(PACK):
+                y_pass(0, s, n)
+        for q in range(QUADS):
+            h_pass(1, q)
+
+        cast_shared(d_views, d_raw[2], d_bf[2])
+        deal_up(0)
+        quantize(d_bf[2], d_codes[2][:], d_scale[2][:])
+        for u in range(2):
+            cast_shared(x_views, x_last_raw[u], x_last_bf[u])
+            quantize(x_last_bf[u], x_codes[2][:, u * HALF : (u + 1) * HALF], x_scale[2][:, u * HALF : (u + 1) * HALF])
+        for q in (0, 1, 3, 2):
+            h_pass(2, q)
+        for s in range(PACK):
+            y_pass(0, s, 2)
+
+        deal_w8(1)
+        h_out_vector(3)
+        for q in range(3):
+            h_out_scalar(q)
+        for u in range(2):
+            quantize(h_bf[u], h_codes[:, u * HALF : (u + 1) * HALF], h_scale[:, u * HALF : (u + 1) * HALF])
+        for s in range(PACK):
+            y_pass(0, s, 3)
+        deal_w4(1)
+        deal_up(1)
+        deal_w8(2)
+        deal_w4(2)
+        deal_up(2)
+
+        for s in range(PACK):
+            y_pass(1, s, 0)
+        for s in range(PACK):
+            for n in range(1, 4):
+                y_pass(1, s, n)
+        for s in range(PACK):
+            relu_scalar(0, s)
+        for s in range(PACK):
+            square(0, s)
+            if s % 2 == 1:
+                store_f32(0, s - 1, s + 1)
+        for s in range(PACK):
+            for n in range(4):
+                y_pass(2, s, n)
+
+        for s in range(2):
+            relu_vector(1, s)
+            square(1, s)
+        store_f32(1, 0, 2)
+        planes(0)
+        store_codes(0, 0, T)
+        for s in range(2, PACK):
+            relu_scalar(1, s)
+            square(1, s)
+        store_f32(1, 2, PACK)
+
+        for s in range(2):
+            relu_vector(2, s)
+            square(2, s)
+        store_f32(2, 0, 2)
+        planes(1)
+        store_codes(1, 0, T)
+        relu_scalar(2, 2)
+        square(2, 2)
+        store_f32(2, 2, 3)
+        relu_vector(2, 3)
+        square(2, 3)
+        store_f32(2, 3, PACK)
+        planes(2)
+        for u in range(2):
+            store_codes(2, u * HALF, (u + 1) * HALF)
+        for q in range(QUADS):
+            store_scale_rows(nc.scalar if q % 2 else nc.sync, q)

@@ -22,6 +22,7 @@ QUADS = 4
 HALF = T // 2
 TQ = T // 4
 W8_ROW = 4
+LAST_PIECES = ((0, 2 * TQ), (2 * TQ, 3 * TQ), (3 * TQ, T))
 
 
 def tile_mix_three_fm_pl_relu2_kernel(
@@ -39,16 +40,16 @@ def tile_mix_three_fm_pl_relu2_kernel(
         banks = [ps.tile([P, T], F32, name="bank%d" % n) for n in range(8)]
 
         x_raw = tiles("x_raw", 2, [P, PACK, T], F32)
-        x_last_raw = tiles("x_last_raw", 2, [P, PACK, HALF], F32)
+        x_last_raw = [sb.tile([P, PACK, hi - lo], F32, name="x_last_raw%d" % lo, align_bytes=64) for lo, hi in LAST_PIECES]
         d_raw = tiles("d_raw", 3, [P, PACK, R], F32)
         x_bf = tiles("x_bf", 2, [P, T * PACK], BF16)
-        x_last_bf = tiles("x_last_bf", 2, [P, HALF * PACK], BF16)
+        x_last_bf = [sb.tile([P, (hi - lo) * PACK], BF16, name="x_last_bf%d" % lo, align_bytes=64) for lo, hi in LAST_PIECES]
         d_bf = tiles("d_bf", 3, [P, R * PACK], BF16)
         x_codes = tiles("x_codes", 3, [P, T], I32)
         x_scale = tiles("x_scale", 3, [P, T], U8)
         d_codes = tiles("d_codes", 3, [P, R], I32)
         d_scale = tiles("d_scale", 3, [P, R], U8)
-        h_bf = tiles("h_bf", 2, [P, HALF * PACK], BF16)
+        h_bf = tiles("h_bf", QUADS, [P, TQ * PACK], BF16)
         h_codes = sb.tile([P, T], I32, align_bytes=64)
         h_scale = sb.tile([P, T], U8, align_bytes=64)
 
@@ -64,7 +65,7 @@ def tile_mix_three_fm_pl_relu2_kernel(
         up8_s = sb.tile([P, M], U8, align_bytes=64)
 
         o_f32 = tiles("o_f32", GROUPS, [P, PACK, T], F32)
-        o_bf = tiles("o_bf", 2 * GROUPS, [P, HALF * PACK], BF16)
+        o_bf = tiles("o_bf", GROUPS, [P, T * PACK], BF16)
         o_codes = tiles("o_codes", GROUPS, [P, T], I32)
         o_scale = sb.tile([P, GROUPS * T], U8, align_bytes=64)
 
@@ -147,7 +148,7 @@ def tile_mix_three_fm_pl_relu2_kernel(
                 )
 
         def h_views(q):
-            dst = h_bf[q // 2][:, (q % 2) * TQ * PACK : (q % 2 + 1) * TQ * PACK].rearrange("p (t s) -> p t s", s=PACK)
+            dst = h_bf[q][:].rearrange("p (t s) -> p t s", s=PACK)
             return dst, banks[4 + q][:].rearrange("p (s t) -> p t s", s=PACK)
 
         def h_out_scalar(q):
@@ -181,32 +182,31 @@ def tile_mix_three_fm_pl_relu2_kernel(
                 stop=(n == 3),
             )
 
-        def relu_scalar(a, s):
-            nc.scalar.activation(out=o_f32[a][:, s, :], in_=y_bank(a, s)[:], func=ACT.Relu)
+        def relu_scalar(a, s, lo=0, hi=T):
+            nc.scalar.activation(out=o_f32[a][:, s, lo:hi], in_=y_bank(a, s)[:, lo:hi], func=ACT.Relu)
 
         def relu_vector(a, s):
             nc.vector.tensor_scalar(out=o_f32[a][:, s, :], in0=y_bank(a, s)[:], scalar1=0.0, scalar2=None, op0=ALU.max)
 
-        def square(a, s):
-            nc.scalar.activation(out=o_f32[a][:, s, :], in_=o_f32[a][:, s, :], func=ACT.Square)
+        def square(a, s, lo=0, hi=T):
+            nc.scalar.activation(out=o_f32[a][:, s, lo:hi], in_=o_f32[a][:, s, lo:hi], func=ACT.Square)
 
-        def out_cast(a, u):
-            dst = o_bf[2 * a + u][:].rearrange("p (c i j) -> p c j i", i=4, j=PACK)
-            src = o_f32[a][:, :, u * HALF : (u + 1) * HALF].rearrange("p j (c i) -> p c j i", i=4)
-            nc.vector.tensor_copy(out=dst, in_=src)
+        def square_vector(a, s, lo=0, hi=T):
+            part = o_f32[a][:, s, lo:hi]
+            nc.vector.tensor_tensor(out=part, in0=part, in1=part, op=ALU.mult)
 
-        def out_quantize(a, u):
-            quantize(
-                o_bf[2 * a + u],
-                o_codes[a][:, u * HALF : (u + 1) * HALF],
-                o_scale[:, a * T + u * HALF : a * T + (u + 1) * HALF],
+        def out_quantize(a, lo, hi):
+            nc.vector.quantize_mx(
+                out=o_codes[a][:, lo:hi].bitcast(FP8X4),
+                scales=o_scale[:, a * T + lo : a * T + hi],
+                in_=o_bf[a][:, lo * PACK : hi * PACK],
             )
 
         def planes(a):
             for u in range(2):
-                out_cast(a, u)
+                cast_vector(x_views, o_f32[a], o_bf[a], u * HALF, (u + 1) * HALF)
             for u in range(2):
-                out_quantize(a, u)
+                out_quantize(a, u * HALF, (u + 1) * HALF)
 
         def store_f32(a, lo, hi):
             nc.sync.dma_start(out=rows(out_0, a)[:, lo:hi, :], in_=o_f32[a][:, lo:hi, :])
@@ -215,86 +215,92 @@ def tile_mix_three_fm_pl_relu2_kernel(
             dst = out_1[a].rearrange("p t i -> p (t i)")[:, lo * PACK : hi * PACK].bitcast(I32)
             nc.sync.dma_start(out=dst, in_=o_codes[a][:, lo:hi])
 
-        def store_scale_rows(queue, q):
-            src = o_scale[32 * q : 32 * q + 4, :].bitcast(I32).rearrange("r (a w) -> r a w", a=GROUPS)
-            queue.dma_start(out=out_2[:, 4 * q : 4 * q + 4, :].rearrange("a r t -> r a t").bitcast(I32), in_=src)
+        def store_scale_rows(queue, q, lo, hi):
+            src = o_scale[32 * q : 32 * q + 4, lo * T : hi * T].bitcast(I32).rearrange("r (a w) -> r a w", a=hi - lo)
+            queue.dma_start(out=out_2[lo:hi, 4 * q : 4 * q + 4, :].rearrange("a r t -> r a t").bitcast(I32), in_=src)
 
-        def load_w4_scale(q):
+        nc.vector.memset(up8_s_raw[:].bitcast(I32), 0)
+        nc.vector.memset(w4_s_raw[:].bitcast(I32), 0)
+        for src, row in ((w8_scales, W8_ROW), (up_scales, 0)):
+            for q in range(QUADS):
+                nc.gpsimd.dma_start(
+                    out=up8_s_raw[32 * q + row : 32 * q + row + 4, :].bitcast(I32),
+                    in_=src[0, 4 * q : 4 * q + 4, :].bitcast(I32),
+                )
+        nc.sync.dma_start(out=x_raw[0][:], in_=rows(x, 0))
+        for q in range(QUADS):
             nc.sync.dma_start(
                 out=w4_s_raw[32 * q : 32 * q + 4].bitcast(I32),
                 in_=w4_scales[:, 4 * q : 4 * q + 4, :].rearrange("g r n -> r g n").bitcast(I32),
             )
-
-        def load_up8_scale(src, row, q):
-            nc.sync.dma_start(
-                out=up8_s_raw[32 * q + row : 32 * q + row + 4, :].bitcast(I32),
-                in_=src[0, 4 * q : 4 * q + 4, :].bitcast(I32),
-            )
-
-        nc.vector.memset(w4_s_raw[:].bitcast(I32), 0)
-        nc.vector.memset(up8_s_raw[:].bitcast(I32), 0)
-        nc.sync.dma_start(out=x_raw[0][:], in_=rows(x, 0))
-        for q in range(QUADS):
-            load_w4_scale(q)
-        for q in range(2):
-            load_up8_scale(w8_scales, W8_ROW, q)
         nc.sync.dma_start(out=d_raw[0][:], in_=rows(down, 0))
-        nc.sync.dma_start(out=x_raw[1][:], in_=rows(x, 1))
-        for q in range(2, QUADS):
-            load_up8_scale(w8_scales, W8_ROW, q)
-        for q in range(QUADS):
-            load_up8_scale(up_scales, 0, q)
-        nc.sync.dma_start(out=d_raw[1][:], in_=rows(down, 1))
         load_w8(0)
         load_w4(0)
         load_up(0)
+        nc.sync.dma_start(out=x_raw[1][:], in_=rows(x, 1))
+        nc.sync.dma_start(out=d_raw[1][:], in_=rows(down, 1))
         nc.sync.dma_start(out=d_raw[2][:], in_=rows(down, 2))
-        for u in range(2):
-            nc.sync.dma_start(out=x_last_raw[u][:], in_=rows(x, 2)[:, :, u * HALF : (u + 1) * HALF])
+        for u, (lo, hi) in enumerate(LAST_PIECES):
+            nc.sync.dma_start(out=x_last_raw[u][:], in_=rows(x, 2)[:, :, lo:hi])
         for a in range(1, GROUPS):
             load_w8(a)
             load_w4(a)
             load_up(a)
 
         cast_scalar(x_views, x_raw[0], x_bf[0], 0, T)
+        cast_scalar(d_views, d_raw[0], d_bf[0], 0, R)
         for g in range(2):
             deal_scale(w4_s[g][:], w4_s_raw[:, g, :])
         quantize(x_bf[0], x_codes[0][:], x_scale[0][:])
-        cast_shared(d_views, d_raw[0], d_bf[0])
-        quantize(d_bf[0], d_codes[0][:], d_scale[0][:])
-        for q in range(QUADS):
-            h_pass(0, q)
-
-        cast_shared(x_views, x_raw[1], x_bf[1])
-        deal_scale(up8_s[:], up8_s_raw[:])
-        quantize(x_bf[1], x_codes[1][:], x_scale[1][:])
-        cast_scalar(d_views, d_raw[1], d_bf[1], 0, R)
         deal_w8(0)
         deal_w4(0)
+        quantize(d_bf[0], d_codes[0][:], d_scale[0][:])
+        deal_up(0)
+        deal_scale(up8_s[:], up8_s_raw[:])
+        for q in range(QUADS):
+            h_pass(0, q)
+        for s in range(PACK):
+            y_pass(0, s, 0)
+
+        cast_shared(x_views, x_raw[1], x_bf[1])
+        quantize(x_bf[1], x_codes[1][:], x_scale[1][:])
+        for s in range(PACK):
+            y_pass(0, s, 1)
+        cast_shared(d_views, d_raw[1], d_bf[1])
         quantize(d_bf[1], d_codes[1][:], d_scale[1][:])
-        for n in range(2):
-            for s in range(PACK):
-                y_pass(0, s, n)
         for q in range(QUADS):
             h_pass(1, q)
 
+        def x_last_quantize(u):
+            lo, hi = LAST_PIECES[u]
+            quantize(x_last_bf[u], x_codes[2][:, lo:hi], x_scale[2][:, lo:hi])
+
         cast_shared(d_views, d_raw[2], d_bf[2])
-        deal_up(0)
         quantize(d_bf[2], d_codes[2][:], d_scale[2][:])
-        for u in range(2):
-            cast_shared(x_views, x_last_raw[u], x_last_bf[u])
-            quantize(x_last_bf[u], x_codes[2][:, u * HALF : (u + 1) * HALF], x_scale[2][:, u * HALF : (u + 1) * HALF])
-        for q in (0, 1, 3, 2):
+        cast_scalar(x_views, x_last_raw[0], x_last_bf[0], 0, 160)
+        cast_vector(x_views, x_last_raw[0], x_last_bf[0], 160, HALF)
+        x_last_quantize(0)
+        cast_scalar(x_views, x_last_raw[1], x_last_bf[1], 0, TQ)
+        x_last_quantize(1)
+        cast_shared(x_views, x_last_raw[2], x_last_bf[2])
+        x_last_quantize(2)
+        for q in range(QUADS):
             h_pass(2, q)
         for s in range(PACK):
             y_pass(0, s, 2)
 
-        deal_w8(1)
-        h_out_vector(3)
-        for q in range(3):
+        def h_quantize(q):
+            quantize(h_bf[q], h_codes[:, q * TQ : (q + 1) * TQ], h_scale[:, q * TQ : (q + 1) * TQ])
+
+        for q in (0, 1, 3):
             h_out_scalar(q)
-        for u in range(2):
-            quantize(h_bf[u], h_codes[:, u * HALF : (u + 1) * HALF], h_scale[:, u * HALF : (u + 1) * HALF])
+        h_out_vector(2)
+        h_quantize(0)
+        deal_w8(1)
+        for q in range(1, QUADS):
+            h_quantize(q)
+        for s in range(2):
+            y_pass(1, s, 0)
         for s in range(PACK):
             y_pass(0, s, 3)
         deal_w4(1)
@@ -303,17 +309,17 @@ def tile_mix_three_fm_pl_relu2_kernel(
         deal_w4(2)
         deal_up(2)
 
-        for s in range(PACK):
+        for s in range(2, PACK):
             y_pass(1, s, 0)
         for s in range(PACK):
             for n in range(1, 4):
                 y_pass(1, s, n)
-        for s in range(PACK):
-            relu_scalar(0, s)
-        for s in range(PACK):
-            square(0, s)
-            if s % 2 == 1:
-                store_f32(0, s - 1, s + 1)
+        for lo in (0, 2):
+            for s in (lo, lo + 1):
+                relu_scalar(0, s)
+            for s in (lo, lo + 1):
+                square(0, s)
+            store_f32(0, lo, lo + 2)
         for s in range(PACK):
             for n in range(4):
                 y_pass(2, s, n)
@@ -326,23 +332,29 @@ def tile_mix_three_fm_pl_relu2_kernel(
         store_codes(0, 0, T)
         for s in range(2, PACK):
             relu_scalar(1, s)
+        for s in range(2, PACK):
             square(1, s)
         store_f32(1, 2, PACK)
 
-        for s in range(2):
+        for s in range(3):
             relu_vector(2, s)
             square(2, s)
         store_f32(2, 0, 2)
         planes(1)
-        store_codes(1, 0, T)
-        relu_scalar(2, 2)
-        square(2, 2)
         store_f32(2, 2, 3)
-        relu_vector(2, 3)
-        square(2, 3)
-        store_f32(2, 3, PACK)
-        planes(2)
+        store_codes(1, 0, T)
+        for q in range(QUADS):
+            store_scale_rows(nc.sync, q, 0, 2)
         for u in range(2):
+            relu_scalar(2, 3, u * HALF, (u + 1) * HALF)
+        for u in range(2):
+            square(2, 3, u * HALF, (u + 1) * HALF)
+        store_f32(2, 3, PACK)
+        cast_vector(x_views, o_f32[2], o_bf[2], 0, HALF)
+        cast_scalar(x_views, o_f32[2], o_bf[2], 3 * TQ, T)
+        cast_vector(x_views, o_f32[2], o_bf[2], HALF, 3 * TQ)
+        for u in range(2):
+            out_quantize(2, u * HALF, (u + 1) * HALF)
             store_codes(2, u * HALF, (u + 1) * HALF)
         for q in range(QUADS):
-            store_scale_rows(nc.scalar if q % 2 else nc.sync, q)
+            store_scale_rows(nc.scalar if q % 2 else nc.sync, q, 2, 3)

@@ -90,8 +90,8 @@ def tile_mix_three_fm_pl_relu2_kernel(
             return dst, src
 
         def d_views(raw, bf, lo, hi):
-            dst = bf[:].rearrange("p (s m j) -> p m j s", s=PACK, j=PACK)[:, lo // PACK : hi // PACK]
-            src = raw[:, :, lo:hi].rearrange("p j (m s) -> p m j s", s=PACK)
+            dst = bf[:].rearrange("p (u v m j) -> p u m j v", u=2, v=2, j=PACK)[:, :, lo // PACK : hi // PACK]
+            src = raw[:, :, lo:hi].rearrange("p j (m u v) -> p u m j v", u=2, v=2)
             return dst, src
 
         def cast_scalar(views, raw, bf, lo, hi):
@@ -119,8 +119,8 @@ def tile_mix_three_fm_pl_relu2_kernel(
 
         def deal_w8(a):
             nc.vector.tensor_copy(
-                out=w8_dealt[a][:].rearrange("p (s m) -> p m s", s=PACK),
-                in_=w8_raw[a][:].rearrange("p (m s) -> p m s", s=PACK),
+                out=w8_dealt[a][:].rearrange("p (u v m) -> p u m v", u=2, v=2),
+                in_=w8_raw[a][:].rearrange("p (m u v) -> p u m v", u=2, v=2),
             )
 
         def deal_w4(a):
@@ -219,26 +219,32 @@ def tile_mix_three_fm_pl_relu2_kernel(
             src = o_scale[32 * q : 32 * q + 4, lo * T : hi * T].bitcast(I32).rearrange("r (a w) -> r a w", a=hi - lo)
             queue.dma_start(out=out_2[lo:hi, 4 * q : 4 * q + 4, :].rearrange("a r t -> r a t").bitcast(I32), in_=src)
 
-        nc.vector.memset(up8_s_raw[:].bitcast(I32), 0)
-        nc.vector.memset(w4_s_raw[:].bitcast(I32), 0)
-        for src, row in ((w8_scales, W8_ROW), (up_scales, 0)):
-            for q in range(QUADS):
-                nc.gpsimd.dma_start(
-                    out=up8_s_raw[32 * q + row : 32 * q + row + 4, :].bitcast(I32),
-                    in_=src[0, 4 * q : 4 * q + 4, :].bitcast(I32),
-                )
-        nc.sync.dma_start(out=x_raw[0][:], in_=rows(x, 0))
-        for q in range(QUADS):
+        def load_w4_scale(r):
             nc.sync.dma_start(
-                out=w4_s_raw[32 * q : 32 * q + 4].bitcast(I32),
-                in_=w4_scales[:, 4 * q : 4 * q + 4, :].rearrange("g r n -> r g n").bitcast(I32),
+                out=w4_s_raw[r:P:32].bitcast(I32),
+                in_=w4_scales[:, r:16:4, :].rearrange("g q n -> q g n").bitcast(I32),
             )
+
+        def load_up8_scale(src, row, r):
+            nc.sync.dma_start(out=up8_s_raw[row + r : P : 32, :].bitcast(I32), in_=src[0, r:16:4, :].bitcast(I32))
+
+        nc.vector.memset(w4_s_raw[:].bitcast(I32), 0)
+        nc.vector.memset(up8_s_raw[:].bitcast(I32), 0)
+        nc.sync.dma_start(out=x_raw[0][:], in_=rows(x, 0))
+        for r in range(4):
+            load_w4_scale(r)
         nc.sync.dma_start(out=d_raw[0][:], in_=rows(down, 0))
+        for r in range(2):
+            load_up8_scale(w8_scales, W8_ROW, r)
         load_w8(0)
         load_w4(0)
-        load_up(0)
+        for r in range(2, 4):
+            load_up8_scale(w8_scales, W8_ROW, r)
         nc.sync.dma_start(out=x_raw[1][:], in_=rows(x, 1))
+        for r in range(4):
+            load_up8_scale(up_scales, 0, r)
         nc.sync.dma_start(out=d_raw[1][:], in_=rows(down, 1))
+        load_up(0)
         nc.sync.dma_start(out=d_raw[2][:], in_=rows(down, 2))
         for u, (lo, hi) in enumerate(LAST_PIECES):
             nc.sync.dma_start(out=x_last_raw[u][:], in_=rows(x, 2)[:, :, lo:hi])
@@ -255,21 +261,21 @@ def tile_mix_three_fm_pl_relu2_kernel(
         deal_w8(0)
         deal_w4(0)
         quantize(d_bf[0], d_codes[0][:], d_scale[0][:])
-        deal_up(0)
-        deal_scale(up8_s[:], up8_s_raw[:])
         for q in range(QUADS):
             h_pass(0, q)
-        for s in range(PACK):
-            y_pass(0, s, 0)
 
         cast_shared(x_views, x_raw[1], x_bf[1])
+        deal_scale(up8_s[:], up8_s_raw[:])
         quantize(x_bf[1], x_codes[1][:], x_scale[1][:])
         for s in range(PACK):
-            y_pass(0, s, 1)
+            y_pass(0, s, 0)
         cast_shared(d_views, d_raw[1], d_bf[1])
+        deal_up(0)
         quantize(d_bf[1], d_codes[1][:], d_scale[1][:])
         for q in range(QUADS):
             h_pass(1, q)
+        for s in range(PACK):
+            y_pass(0, s, 1)
 
         def x_last_quantize(u):
             lo, hi = LAST_PIECES[u]
@@ -343,8 +349,6 @@ def tile_mix_three_fm_pl_relu2_kernel(
         planes(1)
         store_f32(2, 2, 3)
         store_codes(1, 0, T)
-        for q in range(QUADS):
-            store_scale_rows(nc.sync, q, 0, 2)
         for u in range(2):
             relu_scalar(2, 3, u * HALF, (u + 1) * HALF)
         for u in range(2):
@@ -357,4 +361,4 @@ def tile_mix_three_fm_pl_relu2_kernel(
             out_quantize(2, u * HALF, (u + 1) * HALF)
             store_codes(2, u * HALF, (u + 1) * HALF)
         for q in range(QUADS):
-            store_scale_rows(nc.scalar if q % 2 else nc.sync, q, 2, 3)
+            store_scale_rows(nc.scalar if q % 2 else nc.sync, q, 0, 3)

@@ -2,7 +2,7 @@ from contextlib import ExitStack
 
 import concourse.mybir as mybir
 
-O, K, R, M, T = 512, 1536, 512, 1536, 512
+K, R, M, T = 1536, 512, 1536, 512
 FLOPS = 2 * T * (K * R + K * M + R * M)
 
 F32 = mybir.dt.float32
@@ -18,11 +18,16 @@ P = 128
 PACK = 4
 KP = P * PACK
 GROUPS = M // KP
-QUADS = 4
+QUARTERS = 4
 HALF = T // 2
-TQ = T // 4
+TQ = T // QUARTERS
+QUAD = 32
+SCALE_ROWS = 4
 W8_ROW = 4
+UP_PASS = 3
 LAST_PIECES = ((0, 2 * TQ), (2 * TQ, 3 * TQ), (3 * TQ, T))
+FIRST_PIECE_CUT = 160
+LAST_GROUP_CUT = 352
 
 
 def tile_mix_three_fm_pl_relu2_kernel(
@@ -49,7 +54,7 @@ def tile_mix_three_fm_pl_relu2_kernel(
         x_scale = tiles("x_scale", 3, [P, T], U8)
         d_codes = tiles("d_codes", 3, [P, R], I32)
         d_scale = tiles("d_scale", 3, [P, R], U8)
-        h_bf = tiles("h_bf", QUADS, [P, TQ * PACK], BF16)
+        h_bf = tiles("h_bf", QUARTERS, [P, TQ * PACK], BF16)
         h_codes = sb.tile([P, T], I32, align_bytes=64)
         h_scale = sb.tile([P, T], U8, align_bytes=64)
 
@@ -69,6 +74,7 @@ def tile_mix_three_fm_pl_relu2_kernel(
         o_codes = tiles("o_codes", GROUPS, [P, T], I32)
         o_scale = sb.tile([P, GROUPS * T], U8, align_bytes=64)
 
+
         def rows(src, c):
             return src[c * KP : (c + 1) * KP, :].rearrange("(p j) w -> p j w", j=PACK)
 
@@ -84,32 +90,55 @@ def tile_mix_three_fm_pl_relu2_kernel(
         def load_up(a):
             nc.sync.dma_start(out=up_raw[a][:].bitcast(I32), in_=up_words[0][:, a * 2 * KP : (a + 1) * 2 * KP].bitcast(I32))
 
-        def x_views(raw, bf, lo, hi):
+        def load_w4_scale(r):
+            nc.sync.dma_start(
+                out=w4_s_raw[r:P:QUAD].bitcast(I32),
+                in_=w4_scales[:, r:16:SCALE_ROWS, :].rearrange("g q n -> q g n").bitcast(I32),
+            )
+
+        def load_up8_scale(src, first_row, r):
+            nc.sync.dma_start(
+                out=up8_s_raw[first_row + r : P : QUAD, :].bitcast(I32), in_=src[0, r:16:SCALE_ROWS, :].bitcast(I32)
+            )
+
+
+        def plain_views(raw, bf, lo, hi):
             dst = bf[:, lo * PACK : hi * PACK].rearrange("p (c i j) -> p c j i", i=4, j=PACK)
             src = raw[:, :, lo:hi].rearrange("p j (c i) -> p c j i", i=4)
             return dst, src
 
-        def d_views(raw, bf, lo, hi):
+        def dealt_views(raw, bf, lo, hi):
             dst = bf[:].rearrange("p (u v m j) -> p u m j v", u=2, v=2, j=PACK)[:, :, lo // PACK : hi // PACK]
             src = raw[:, :, lo:hi].rearrange("p j (m u v) -> p u m j v", u=2, v=2)
             return dst, src
 
-        def cast_scalar(views, raw, bf, lo, hi):
+        def round_scalar(views, raw, bf, lo, hi):
             dst, src = views(raw, bf, lo, hi)
             nc.scalar.copy(out=dst, in_=src)
 
-        def cast_vector(views, raw, bf, lo, hi):
+        def round_vector(views, raw, bf, lo, hi):
             dst, src = views(raw, bf, lo, hi)
             nc.vector.tensor_copy(out=dst, in_=src)
 
-        def cast_shared(views, raw, bf):
+        def round_shared(views, raw, bf):
             width = raw.shape[2]
             cut = 3 * width // 8
-            cast_scalar(views, raw, bf, 0, cut)
-            cast_vector(views, raw, bf, cut, width)
+            round_scalar(views, raw, bf, 0, cut)
+            round_vector(views, raw, bf, cut, width)
 
         def quantize(bf, codes, scale):
-            nc.vector.quantize_mx(out=codes.bitcast(FP8X4), scales=scale, in_=bf[:])
+            nc.vector.quantize_mx(out=codes.bitcast(FP8X4), scales=scale, in_=bf)
+
+        def quantize_x(c):
+            quantize(x_bf[c][:], x_codes[c][:], x_scale[c][:])
+
+        def quantize_x_last(u):
+            lo, hi = LAST_PIECES[u]
+            quantize(x_last_bf[u][:], x_codes[2][:, lo:hi], x_scale[2][:, lo:hi])
+
+        def quantize_down(c):
+            quantize(d_bf[c][:], d_codes[c][:], d_scale[c][:])
+
 
         def deal_scale(dst, src):
             nc.vector.tensor_copy(
@@ -135,6 +164,7 @@ def tile_mix_three_fm_pl_relu2_kernel(
                 in_=up_raw[a][:].rearrange("p (m s b) -> p s m b", s=PACK, b=2),
             )
 
+
         def h_pass(c, q):
             for s in range(PACK):
                 nc.tensor.matmul_mx(
@@ -148,30 +178,33 @@ def tile_mix_three_fm_pl_relu2_kernel(
                 )
 
         def h_views(q):
-            dst = h_bf[q][:].rearrange("p (t s) -> p t s", s=PACK)
-            return dst, banks[4 + q][:].rearrange("p (s t) -> p t s", s=PACK)
+            return h_bf[q][:].rearrange("p (t s) -> p t s", s=PACK), banks[4 + q][:].rearrange("p (s t) -> p t s", s=PACK)
 
-        def h_out_scalar(q):
+        def round_h_scalar(q):
             dst, src = h_views(q)
             nc.scalar.copy(out=dst, in_=src)
 
-        def h_out_vector(q):
+        def round_h_vector(q):
             dst, src = h_views(q)
             nc.vector.tensor_copy(out=dst, in_=src)
+
+        def quantize_h(q):
+            quantize(h_bf[q][:], h_codes[:, q * TQ : (q + 1) * TQ], h_scale[:, q * TQ : (q + 1) * TQ])
+
 
         def y_bank(a, s):
             return banks[4 * (a % 2) + s]
 
         def y_pass(a, s, n):
             cols = slice(a * KP + s * P, a * KP + (s + 1) * P)
-            pair = slice(2 * s * P, 2 * (s + 1) * P)
+            fp4_bytes = slice(2 * s * P, 2 * (s + 1) * P)
             if n == 0:
                 lhs, lhs_scale = w8_dealt[a][:, s * P : (s + 1) * P].bitcast(FP8X4), up8_s[W8_ROW:P, cols]
-            elif n < 3:
-                lhs, lhs_scale = w4_dealt[a][:, n - 1, pair].bitcast(FP4X4), w4_s[n - 1][:, cols]
+            elif n < UP_PASS:
+                lhs, lhs_scale = w4_dealt[a][:, n - 1, fp4_bytes].bitcast(FP4X4), w4_s[n - 1][:, cols]
             else:
-                lhs, lhs_scale = up_dealt[a][:, pair].bitcast(FP4X4), up8_s[:, cols]
-            codes, scale = (x_codes[n], x_scale[n]) if n < 3 else (h_codes, h_scale)
+                lhs, lhs_scale = up_dealt[a][:, fp4_bytes].bitcast(FP4X4), up8_s[:, cols]
+            codes, scale = (x_codes[n], x_scale[n]) if n < UP_PASS else (h_codes, h_scale)
             nc.tensor.matmul_mx(
                 out=y_bank(a, s)[:],
                 lhsT=lhs,
@@ -179,7 +212,7 @@ def tile_mix_three_fm_pl_relu2_kernel(
                 rhs=codes[:].bitcast(FP8X4),
                 rhs_scale=scale[:],
                 start=(n == 0),
-                stop=(n == 3),
+                stop=(n == UP_PASS),
             )
 
         def relu_scalar(a, s, lo=0, hi=T):
@@ -191,22 +224,15 @@ def tile_mix_three_fm_pl_relu2_kernel(
         def square(a, s, lo=0, hi=T):
             nc.scalar.activation(out=o_f32[a][:, s, lo:hi], in_=o_f32[a][:, s, lo:hi], func=ACT.Square)
 
-        def square_vector(a, s, lo=0, hi=T):
-            part = o_f32[a][:, s, lo:hi]
-            nc.vector.tensor_tensor(out=part, in0=part, in1=part, op=ALU.mult)
-
-        def out_quantize(a, lo, hi):
-            nc.vector.quantize_mx(
-                out=o_codes[a][:, lo:hi].bitcast(FP8X4),
-                scales=o_scale[:, a * T + lo : a * T + hi],
-                in_=o_bf[a][:, lo * PACK : hi * PACK],
-            )
+        def quantize_out(a, u):
+            lo, hi = u * HALF, (u + 1) * HALF
+            quantize(o_bf[a][:, lo * PACK : hi * PACK], o_codes[a][:, lo:hi], o_scale[:, a * T + lo : a * T + hi])
 
         def planes(a):
             for u in range(2):
-                cast_vector(x_views, o_f32[a], o_bf[a], u * HALF, (u + 1) * HALF)
+                round_vector(plain_views, o_f32[a], o_bf[a], u * HALF, (u + 1) * HALF)
             for u in range(2):
-                out_quantize(a, u * HALF, (u + 1) * HALF)
+                quantize_out(a, u)
 
         def store_f32(a, lo, hi):
             nc.sync.dma_start(out=rows(out_0, a)[:, lo:hi, :], in_=o_f32[a][:, lo:hi, :])
@@ -215,33 +241,27 @@ def tile_mix_three_fm_pl_relu2_kernel(
             dst = out_1[a].rearrange("p t i -> p (t i)")[:, lo * PACK : hi * PACK].bitcast(I32)
             nc.sync.dma_start(out=dst, in_=o_codes[a][:, lo:hi])
 
-        def store_scale_rows(queue, q, lo, hi):
-            src = o_scale[32 * q : 32 * q + 4, lo * T : hi * T].bitcast(I32).rearrange("r (a w) -> r a w", a=hi - lo)
-            queue.dma_start(out=out_2[lo:hi, 4 * q : 4 * q + 4, :].rearrange("a r t -> r a t").bitcast(I32), in_=src)
+        def store_scale_rows(queue, quad):
+            src = o_scale[QUAD * quad : QUAD * quad + SCALE_ROWS, :].bitcast(I32).rearrange("r (a w) -> r a w", a=GROUPS)
+            dst = out_2[:, SCALE_ROWS * quad : SCALE_ROWS * (quad + 1), :].rearrange("a r t -> r a t").bitcast(I32)
+            queue.dma_start(out=dst, in_=src)
 
-        def load_w4_scale(r):
-            nc.sync.dma_start(
-                out=w4_s_raw[r:P:32].bitcast(I32),
-                in_=w4_scales[:, r:16:4, :].rearrange("g q n -> q g n").bitcast(I32),
-            )
-
-        def load_up8_scale(src, row, r):
-            nc.sync.dma_start(out=up8_s_raw[row + r : P : 32, :].bitcast(I32), in_=src[0, r:16:4, :].bitcast(I32))
 
         nc.vector.memset(w4_s_raw[:].bitcast(I32), 0)
         nc.vector.memset(up8_s_raw[:].bitcast(I32), 0)
+
         nc.sync.dma_start(out=x_raw[0][:], in_=rows(x, 0))
-        for r in range(4):
+        for r in range(SCALE_ROWS):
             load_w4_scale(r)
         nc.sync.dma_start(out=d_raw[0][:], in_=rows(down, 0))
         for r in range(2):
             load_up8_scale(w8_scales, W8_ROW, r)
         load_w8(0)
         load_w4(0)
-        for r in range(2, 4):
+        for r in range(2, SCALE_ROWS):
             load_up8_scale(w8_scales, W8_ROW, r)
         nc.sync.dma_start(out=x_raw[1][:], in_=rows(x, 1))
-        for r in range(4):
+        for r in range(SCALE_ROWS):
             load_up8_scale(up_scales, 0, r)
         nc.sync.dma_start(out=d_raw[1][:], in_=rows(down, 1))
         load_up(0)
@@ -253,73 +273,65 @@ def tile_mix_three_fm_pl_relu2_kernel(
             load_w4(a)
             load_up(a)
 
-        cast_scalar(x_views, x_raw[0], x_bf[0], 0, T)
-        cast_scalar(d_views, d_raw[0], d_bf[0], 0, R)
+        round_scalar(plain_views, x_raw[0], x_bf[0], 0, T)
+        round_scalar(dealt_views, d_raw[0], d_bf[0], 0, R)
         for g in range(2):
             deal_scale(w4_s[g][:], w4_s_raw[:, g, :])
-        quantize(x_bf[0], x_codes[0][:], x_scale[0][:])
+        quantize_x(0)
         deal_w8(0)
         deal_w4(0)
-        quantize(d_bf[0], d_codes[0][:], d_scale[0][:])
-        for q in range(QUADS):
+        quantize_down(0)
+        for q in range(QUARTERS):
             h_pass(0, q)
 
-        cast_shared(x_views, x_raw[1], x_bf[1])
+        round_shared(plain_views, x_raw[1], x_bf[1])
         deal_scale(up8_s[:], up8_s_raw[:])
-        quantize(x_bf[1], x_codes[1][:], x_scale[1][:])
+        quantize_x(1)
         for s in range(PACK):
             y_pass(0, s, 0)
-        cast_shared(d_views, d_raw[1], d_bf[1])
+        round_shared(dealt_views, d_raw[1], d_bf[1])
         deal_up(0)
-        quantize(d_bf[1], d_codes[1][:], d_scale[1][:])
-        for q in range(QUADS):
+        quantize_down(1)
+        for q in range(QUARTERS):
             h_pass(1, q)
         for s in range(PACK):
             y_pass(0, s, 1)
 
-        def x_last_quantize(u):
-            lo, hi = LAST_PIECES[u]
-            quantize(x_last_bf[u], x_codes[2][:, lo:hi], x_scale[2][:, lo:hi])
-
-        cast_shared(d_views, d_raw[2], d_bf[2])
-        quantize(d_bf[2], d_codes[2][:], d_scale[2][:])
-        cast_scalar(x_views, x_last_raw[0], x_last_bf[0], 0, 160)
-        cast_vector(x_views, x_last_raw[0], x_last_bf[0], 160, HALF)
-        x_last_quantize(0)
-        cast_scalar(x_views, x_last_raw[1], x_last_bf[1], 0, TQ)
-        x_last_quantize(1)
-        cast_shared(x_views, x_last_raw[2], x_last_bf[2])
-        x_last_quantize(2)
-        for q in range(QUADS):
+        round_shared(dealt_views, d_raw[2], d_bf[2])
+        quantize_down(2)
+        round_scalar(plain_views, x_last_raw[0], x_last_bf[0], 0, FIRST_PIECE_CUT)
+        round_vector(plain_views, x_last_raw[0], x_last_bf[0], FIRST_PIECE_CUT, HALF)
+        quantize_x_last(0)
+        round_scalar(plain_views, x_last_raw[1], x_last_bf[1], 0, TQ)
+        quantize_x_last(1)
+        round_shared(plain_views, x_last_raw[2], x_last_bf[2])
+        quantize_x_last(2)
+        for q in range(QUARTERS):
             h_pass(2, q)
         for s in range(PACK):
             y_pass(0, s, 2)
 
-        def h_quantize(q):
-            quantize(h_bf[q], h_codes[:, q * TQ : (q + 1) * TQ], h_scale[:, q * TQ : (q + 1) * TQ])
-
         for q in (0, 1, 3):
-            h_out_scalar(q)
-        h_out_vector(2)
-        h_quantize(0)
+            round_h_scalar(q)
         deal_w8(1)
-        for q in range(1, QUADS):
-            h_quantize(q)
-        for s in range(2):
-            y_pass(1, s, 0)
+        round_h_vector(2)
+        for q in range(QUARTERS):
+            quantize_h(q)
+        y_pass(1, 0, 0)
         for s in range(PACK):
-            y_pass(0, s, 3)
+            y_pass(0, s, UP_PASS)
         deal_w4(1)
         deal_up(1)
         deal_w8(2)
         deal_w4(2)
         deal_up(2)
 
-        for s in range(2, PACK):
+        for s in range(1, PACK):
             y_pass(1, s, 0)
         for s in range(PACK):
-            for n in range(1, 4):
+            for n in range(1, UP_PASS + 1):
                 y_pass(1, s, n)
+
         for lo in (0, 2):
             for s in (lo, lo + 1):
                 relu_scalar(0, s)
@@ -327,7 +339,7 @@ def tile_mix_three_fm_pl_relu2_kernel(
                 square(0, s)
             store_f32(0, lo, lo + 2)
         for s in range(PACK):
-            for n in range(4):
+            for n in range(UP_PASS + 1):
                 y_pass(2, s, n)
 
         for s in range(2):
@@ -342,23 +354,25 @@ def tile_mix_three_fm_pl_relu2_kernel(
             square(1, s)
         store_f32(1, 2, PACK)
 
-        for s in range(3):
+        last = PACK - 1
+        for s in range(last):
             relu_vector(2, s)
             square(2, s)
         store_f32(2, 0, 2)
         planes(1)
-        store_f32(2, 2, 3)
+        store_f32(2, 2, last)
         store_codes(1, 0, T)
+
         for u in range(2):
-            relu_scalar(2, 3, u * HALF, (u + 1) * HALF)
+            relu_scalar(2, last, u * HALF, (u + 1) * HALF)
         for u in range(2):
-            square(2, 3, u * HALF, (u + 1) * HALF)
-        store_f32(2, 3, PACK)
-        cast_vector(x_views, o_f32[2], o_bf[2], 0, HALF)
-        cast_scalar(x_views, o_f32[2], o_bf[2], 3 * TQ, T)
-        cast_vector(x_views, o_f32[2], o_bf[2], HALF, 3 * TQ)
+            square(2, last, u * HALF, (u + 1) * HALF)
+        store_f32(2, last, PACK)
+        round_vector(plain_views, o_f32[2], o_bf[2], 0, HALF)
+        round_scalar(plain_views, o_f32[2], o_bf[2], LAST_GROUP_CUT, T)
+        round_vector(plain_views, o_f32[2], o_bf[2], HALF, LAST_GROUP_CUT)
         for u in range(2):
-            out_quantize(2, u * HALF, (u + 1) * HALF)
+            quantize_out(2, u)
             store_codes(2, u * HALF, (u + 1) * HALF)
-        for q in range(QUADS):
-            store_scale_rows(nc.scalar if q % 2 else nc.sync, q, 0, 3)
+        for quad in range(P // QUAD):
+            store_scale_rows(nc.scalar if quad % 2 else nc.sync, quad)

from contextlib import ExitStack

import concourse.mybir as mybir

K, R, M, T = 1536, 512, 1536, 512
FLOPS = 2 * T * (K * R + K * M + R * M)

F32 = mybir.dt.float32
BF16 = mybir.dt.bfloat16
I32 = mybir.dt.int32
U8 = mybir.dt.uint8
FP8X4 = mybir.dt.float8_e4m3fn_x4
FP4X4 = mybir.dt.float4_e2m1fn_x4
ACT = mybir.ActivationFunctionType
ALU = mybir.AluOpType

P = 128
PACK = 4
KP = P * PACK
GROUPS = M // KP
QUARTERS = 4
HALF = T // 2
TQ = T // QUARTERS
QUAD = 32
SCALE_ROWS = 4
W8_ROW = 4
UP_PASS = 3
LAST_PIECES = ((0, 2 * TQ), (2 * TQ, 3 * TQ), (3 * TQ, T))
FIRST_PIECE_CUT = 160
LAST_GROUP_CUT = 352


def tile_mix_three_fm_pl_relu2_kernel(
    tc, x, w8_words, w8_scales, w4_words, w4_scales, down, up_words, up_scales, out_0, out_1, out_2
):
    nc = tc.nc
    with ExitStack() as ctx:
        sb = ctx.enter_context(tc.tile_pool(name="sb", bufs=1))
        ps = ctx.enter_context(tc.psum_pool(name="ps", bufs=1))
        ctx.enter_context(tc.manual_schedule())

        def tiles(name, count, shape, dtype):
            return [sb.tile(shape, dtype, name="%s%d" % (name, n), align_bytes=64) for n in range(count)]

        banks = [ps.tile([P, T], F32, name="bank%d" % n) for n in range(8)]

        x_raw = tiles("x_raw", 2, [P, PACK, T], F32)
        x_last_raw = [sb.tile([P, PACK, hi - lo], F32, name="x_last_raw%d" % lo, align_bytes=64) for lo, hi in LAST_PIECES]
        d_raw = tiles("d_raw", 3, [P, PACK, R], F32)
        x_bf = tiles("x_bf", 2, [P, T * PACK], BF16)
        x_last_bf = [sb.tile([P, (hi - lo) * PACK], BF16, name="x_last_bf%d" % lo, align_bytes=64) for lo, hi in LAST_PIECES]
        d_bf = tiles("d_bf", 3, [P, R * PACK], BF16)
        x_codes = tiles("x_codes", 3, [P, T], I32)
        x_scale = tiles("x_scale", 3, [P, T], U8)
        d_codes = tiles("d_codes", 3, [P, R], I32)
        d_scale = tiles("d_scale", 3, [P, R], U8)
        h_bf = tiles("h_bf", QUARTERS, [P, TQ * PACK], BF16)
        h_codes = sb.tile([P, T], I32, align_bytes=64)
        h_scale = sb.tile([P, T], U8, align_bytes=64)

        w8_raw = tiles("w8_raw", GROUPS, [P, KP], I32)
        w4_raw = tiles("w4_raw", GROUPS, [P, 2, 2 * KP], U8)
        up_raw = tiles("up_raw", GROUPS, [P, 2 * KP], U8)
        w8_dealt = tiles("w8_dealt", GROUPS, [P, KP], I32)
        w4_dealt = tiles("w4_dealt", GROUPS, [P, 2, 2 * KP], U8)
        up_dealt = tiles("up_dealt", GROUPS, [P, 2 * KP], U8)
        w4_s_raw = sb.tile([P, 2, M], U8, align_bytes=64)
        up8_s_raw = sb.tile([P, M], U8, align_bytes=64)
        w4_s = tiles("w4_s", 2, [P, M], U8)
        up8_s = sb.tile([P, M], U8, align_bytes=64)

        o_f32 = tiles("o_f32", GROUPS, [P, PACK, T], F32)
        o_bf = tiles("o_bf", GROUPS, [P, T * PACK], BF16)
        o_codes = tiles("o_codes", GROUPS, [P, T], I32)
        o_scale = sb.tile([P, GROUPS * T], U8, align_bytes=64)


        def rows(src, c):
            return src[c * KP : (c + 1) * KP, :].rearrange("(p j) w -> p j w", j=PACK)

        w8_src = w8_words[0].rearrange("p n i -> p (n i)")
        w4_src = w4_words.rearrange("g p b -> p g b")

        def load_w8(a):
            nc.sync.dma_start(out=w8_raw[a][:], in_=w8_src[:, a * 4 * KP : (a + 1) * 4 * KP].bitcast(I32))

        def load_w4(a):
            nc.sync.dma_start(out=w4_raw[a][:].bitcast(I32), in_=w4_src[:, :, a * 2 * KP : (a + 1) * 2 * KP].bitcast(I32))

        def load_up(a):
            nc.sync.dma_start(out=up_raw[a][:].bitcast(I32), in_=up_words[0][:, a * 2 * KP : (a + 1) * 2 * KP].bitcast(I32))

        def load_w4_scale(r):
            nc.sync.dma_start(
                out=w4_s_raw[r:P:QUAD].bitcast(I32),
                in_=w4_scales[:, r:16:SCALE_ROWS, :].rearrange("g q n -> q g n").bitcast(I32),
            )

        def load_up8_scale(src, first_row, r):
            nc.sync.dma_start(
                out=up8_s_raw[first_row + r : P : QUAD, :].bitcast(I32), in_=src[0, r:16:SCALE_ROWS, :].bitcast(I32)
            )


        def plain_views(raw, bf, lo, hi):
            dst = bf[:, lo * PACK : hi * PACK].rearrange("p (c i j) -> p c j i", i=4, j=PACK)
            src = raw[:, :, lo:hi].rearrange("p j (c i) -> p c j i", i=4)
            return dst, src

        def dealt_views(raw, bf, lo, hi):
            dst = bf[:].rearrange("p (u v m j) -> p u m j v", u=2, v=2, j=PACK)[:, :, lo // PACK : hi // PACK]
            src = raw[:, :, lo:hi].rearrange("p j (m u v) -> p u m j v", u=2, v=2)
            return dst, src

        def round_scalar(views, raw, bf, lo, hi):
            dst, src = views(raw, bf, lo, hi)
            nc.scalar.copy(out=dst, in_=src)

        def round_vector(views, raw, bf, lo, hi):
            dst, src = views(raw, bf, lo, hi)
            nc.vector.tensor_copy(out=dst, in_=src)

        def round_shared(views, raw, bf):
            width = raw.shape[2]
            cut = 3 * width // 8
            round_scalar(views, raw, bf, 0, cut)
            round_vector(views, raw, bf, cut, width)

        def quantize(bf, codes, scale):
            nc.vector.quantize_mx(out=codes.bitcast(FP8X4), scales=scale, in_=bf)

        def quantize_x(c):
            quantize(x_bf[c][:], x_codes[c][:], x_scale[c][:])

        def quantize_x_last(u):
            lo, hi = LAST_PIECES[u]
            quantize(x_last_bf[u][:], x_codes[2][:, lo:hi], x_scale[2][:, lo:hi])

        def quantize_down(c):
            quantize(d_bf[c][:], d_codes[c][:], d_scale[c][:])


        def deal_scale(dst, src):
            nc.vector.tensor_copy(
                out=dst.rearrange("p (a s m) -> p s a m", a=GROUPS, s=PACK),
                in_=src.rearrange("p (a m s) -> p s a m", a=GROUPS, s=PACK),
            )

        def deal_w8(a):
            nc.vector.tensor_copy(
                out=w8_dealt[a][:].rearrange("p (u v m) -> p u m v", u=2, v=2),
                in_=w8_raw[a][:].rearrange("p (m u v) -> p u m v", u=2, v=2),
            )

        def deal_w4(a):
            nc.vector.tensor_copy(
                out=w4_dealt[a][:].rearrange("p g (s m b) -> p g s m b", s=PACK, b=2),
                in_=w4_raw[a][:].rearrange("p g (m s b) -> p g s m b", s=PACK, b=2),
            )

        def deal_up(a):
            nc.vector.tensor_copy(
                out=up_dealt[a][:].rearrange("p (s m b) -> p s m b", s=PACK, b=2),
                in_=up_raw[a][:].rearrange("p (m s b) -> p s m b", s=PACK, b=2),
            )


        def h_pass(c, q):
            for s in range(PACK):
                nc.tensor.matmul_mx(
                    out=banks[4 + q][:, s * P : (s + 1) * P],
                    lhsT=d_codes[c][:, s * P : (s + 1) * P].bitcast(FP8X4),
                    lhsT_scale=d_scale[c][:, s * P : (s + 1) * P],
                    rhs=x_codes[c][:, q * TQ : (q + 1) * TQ].bitcast(FP8X4),
                    rhs_scale=x_scale[c][:, q * TQ : (q + 1) * TQ],
                    start=(c == 0 and s == 0),
                    stop=(c == 2 and s == PACK - 1),
                )

        def h_views(q):
            return h_bf[q][:].rearrange("p (t s) -> p t s", s=PACK), banks[4 + q][:].rearrange("p (s t) -> p t s", s=PACK)

        def round_h_scalar(q):
            dst, src = h_views(q)
            nc.scalar.copy(out=dst, in_=src)

        def round_h_vector(q):
            dst, src = h_views(q)
            nc.vector.tensor_copy(out=dst, in_=src)

        def quantize_h(q):
            quantize(h_bf[q][:], h_codes[:, q * TQ : (q + 1) * TQ], h_scale[:, q * TQ : (q + 1) * TQ])


        def y_bank(a, s):
            return banks[4 * (a % 2) + s]

        def y_pass(a, s, n):
            cols = slice(a * KP + s * P, a * KP + (s + 1) * P)
            fp4_bytes = slice(2 * s * P, 2 * (s + 1) * P)
            if n == 0:
                lhs, lhs_scale = w8_dealt[a][:, s * P : (s + 1) * P].bitcast(FP8X4), up8_s[W8_ROW:P, cols]
            elif n < UP_PASS:
                lhs, lhs_scale = w4_dealt[a][:, n - 1, fp4_bytes].bitcast(FP4X4), w4_s[n - 1][:, cols]
            else:
                lhs, lhs_scale = up_dealt[a][:, fp4_bytes].bitcast(FP4X4), up8_s[:, cols]
            codes, scale = (x_codes[n], x_scale[n]) if n < UP_PASS else (h_codes, h_scale)
            nc.tensor.matmul_mx(
                out=y_bank(a, s)[:],
                lhsT=lhs,
                lhsT_scale=lhs_scale,
                rhs=codes[:].bitcast(FP8X4),
                rhs_scale=scale[:],
                start=(n == 0),
                stop=(n == UP_PASS),
            )

        def relu_scalar(a, s, lo=0, hi=T):
            nc.scalar.activation(out=o_f32[a][:, s, lo:hi], in_=y_bank(a, s)[:, lo:hi], func=ACT.Relu)

        def relu_vector(a, s):
            nc.vector.tensor_scalar(out=o_f32[a][:, s, :], in0=y_bank(a, s)[:], scalar1=0.0, scalar2=None, op0=ALU.max)

        def square(a, s, lo=0, hi=T):
            nc.scalar.activation(out=o_f32[a][:, s, lo:hi], in_=o_f32[a][:, s, lo:hi], func=ACT.Square)

        def quantize_out(a, u):
            lo, hi = u * HALF, (u + 1) * HALF
            quantize(o_bf[a][:, lo * PACK : hi * PACK], o_codes[a][:, lo:hi], o_scale[:, a * T + lo : a * T + hi])

        def planes(a):
            for u in range(2):
                round_vector(plain_views, o_f32[a], o_bf[a], u * HALF, (u + 1) * HALF)
            for u in range(2):
                quantize_out(a, u)

        def store_f32(a, lo, hi):
            nc.sync.dma_start(out=rows(out_0, a)[:, lo:hi, :], in_=o_f32[a][:, lo:hi, :])

        def store_codes(a, lo, hi):
            dst = out_1[a].rearrange("p t i -> p (t i)")[:, lo * PACK : hi * PACK].bitcast(I32)
            nc.sync.dma_start(out=dst, in_=o_codes[a][:, lo:hi])

        def store_scale_rows(queue, quad):
            src = o_scale[QUAD * quad : QUAD * quad + SCALE_ROWS, :].bitcast(I32).rearrange("r (a w) -> r a w", a=GROUPS)
            dst = out_2[:, SCALE_ROWS * quad : SCALE_ROWS * (quad + 1), :].rearrange("a r t -> r a t").bitcast(I32)
            queue.dma_start(out=dst, in_=src)


        nc.vector.memset(w4_s_raw[:].bitcast(I32), 0)
        nc.vector.memset(up8_s_raw[:].bitcast(I32), 0)

        nc.sync.dma_start(out=x_raw[0][:], in_=rows(x, 0))
        for r in range(SCALE_ROWS):
            load_w4_scale(r)
        nc.sync.dma_start(out=d_raw[0][:], in_=rows(down, 0))
        for r in range(2):
            load_up8_scale(w8_scales, W8_ROW, r)
        load_w8(0)
        load_w4(0)
        for r in range(2, SCALE_ROWS):
            load_up8_scale(w8_scales, W8_ROW, r)
        nc.sync.dma_start(out=x_raw[1][:], in_=rows(x, 1))
        for r in range(SCALE_ROWS):
            load_up8_scale(up_scales, 0, r)
        nc.sync.dma_start(out=d_raw[1][:], in_=rows(down, 1))
        load_up(0)
        nc.sync.dma_start(out=d_raw[2][:], in_=rows(down, 2))
        for u, (lo, hi) in enumerate(LAST_PIECES):
            nc.sync.dma_start(out=x_last_raw[u][:], in_=rows(x, 2)[:, :, lo:hi])
        for a in range(1, GROUPS):
            load_w8(a)
            load_w4(a)
            load_up(a)

        round_scalar(plain_views, x_raw[0], x_bf[0], 0, T)
        round_scalar(dealt_views, d_raw[0], d_bf[0], 0, R)
        for g in range(2):
            deal_scale(w4_s[g][:], w4_s_raw[:, g, :])
        quantize_x(0)
        deal_w8(0)
        deal_w4(0)
        quantize_down(0)
        for q in range(QUARTERS):
            h_pass(0, q)

        round_shared(plain_views, x_raw[1], x_bf[1])
        deal_scale(up8_s[:], up8_s_raw[:])
        quantize_x(1)
        for s in range(PACK):
            y_pass(0, s, 0)
        round_shared(dealt_views, d_raw[1], d_bf[1])
        deal_up(0)
        quantize_down(1)
        for q in range(QUARTERS):
            h_pass(1, q)
        for s in range(PACK):
            y_pass(0, s, 1)

        round_shared(dealt_views, d_raw[2], d_bf[2])
        quantize_down(2)
        round_scalar(plain_views, x_last_raw[0], x_last_bf[0], 0, FIRST_PIECE_CUT)
        round_vector(plain_views, x_last_raw[0], x_last_bf[0], FIRST_PIECE_CUT, HALF)
        quantize_x_last(0)
        round_scalar(plain_views, x_last_raw[1], x_last_bf[1], 0, TQ)
        quantize_x_last(1)
        round_shared(plain_views, x_last_raw[2], x_last_bf[2])
        quantize_x_last(2)
        for q in range(QUARTERS):
            h_pass(2, q)
        for s in range(PACK):
            y_pass(0, s, 2)

        for q in (0, 1, 3):
            round_h_scalar(q)
        deal_w8(1)
        round_h_vector(2)
        for q in range(QUARTERS):
            quantize_h(q)
        y_pass(1, 0, 0)
        for s in range(PACK):
            y_pass(0, s, UP_PASS)
        deal_w4(1)
        deal_up(1)
        deal_w8(2)
        deal_w4(2)
        deal_up(2)

        for s in range(1, PACK):
            y_pass(1, s, 0)
        for s in range(PACK):
            for n in range(1, UP_PASS + 1):
                y_pass(1, s, n)

        for lo in (0, 2):
            for s in (lo, lo + 1):
                relu_scalar(0, s)
            for s in (lo, lo + 1):
                square(0, s)
            store_f32(0, lo, lo + 2)
        for s in range(PACK):
            for n in range(UP_PASS + 1):
                y_pass(2, s, n)

        for s in range(2):
            relu_vector(1, s)
            square(1, s)
        store_f32(1, 0, 2)
        planes(0)
        store_codes(0, 0, T)
        for s in range(2, PACK):
            relu_scalar(1, s)
        for s in range(2, PACK):
            square(1, s)
        store_f32(1, 2, PACK)

        last = PACK - 1
        for s in range(last):
            relu_vector(2, s)
            square(2, s)
        store_f32(2, 0, 2)
        planes(1)
        store_f32(2, 2, last)
        store_codes(1, 0, T)

        for u in range(2):
            relu_scalar(2, last, u * HALF, (u + 1) * HALF)
        for u in range(2):
            square(2, last, u * HALF, (u + 1) * HALF)
        store_f32(2, last, PACK)
        round_vector(plain_views, o_f32[2], o_bf[2], 0, HALF)
        round_scalar(plain_views, o_f32[2], o_bf[2], LAST_GROUP_CUT, T)
        round_vector(plain_views, o_f32[2], o_bf[2], HALF, LAST_GROUP_CUT)
        for u in range(2):
            quantize_out(2, u)
            store_codes(2, u * HALF, (u + 1) * HALF)
        for quad in range(P // QUAD):
            store_scale_rows(nc.scalar if quad % 2 else nc.sync, quad)
